import numpy as np
import ml_dtypes

BF16 = ml_dtypes.bfloat16


def bf(x):
    return np.asarray(x, np.float32).astype(BF16)


def f32(x):
    return np.asarray(x, np.float32)


def f64(x):
    return np.asarray(x).astype(np.float64)


def striped(idx):
    return np.tile(idx.reshape(-1, 16).T, (8, 1))


def rows(idx, k):
    return np.tile(idx, (k, 1))


def look(tab, idx):
    return np.take_along_axis(f64(tab), rows(idx, len(tab)), axis=1)


K, S, V, N = 128, 2048, 1536, 1536


def setup_inputs():
    return {"tab": f32(np.random.standard_normal((K, S))), "pos": f32(np.random.standard_normal((K, V))), "offs": striped(np.random.permutation(S)[:N])}


def reference(tab, pos, offs):
    idx = offs[:16].T.reshape(-1)
    x = np.maximum(look(tab, idx) - f64(pos) + 0.5, 0.0)
    return x

@@ -1,0 +1,29 @@
+import concourse.mybir as mybir
+
+F32, U16 = mybir.dt.float32, mybir.dt.uint16
+MARGIN = 0.5
+PIECE = 512
+PER_COLUMN = 16
+
+
+def tile_lookup_hinge_sub_out_kernel(tc, tab, pos, offs, out):
+    nc = tc.nc
+    rows, width = tab.shape
+    count = pos.shape[1]
+    with tc.tile_pool(name="held", bufs=1) as held:
+        offsets = held.tile([rows, count // PER_COLUMN], U16, name="offsets")
+        table = held.tile([rows, width], F32, name="table")
+        margin = held.tile([rows, 1], F32, name="margin")
+        nc.sync.dma_start(offsets[:], offs)
+        nc.sync.dma_start(table[:], tab)
+        nc.vector.memset(margin[:], MARGIN)
+        for start in range(0, count, PIECE):
+            stop = start + PIECE
+            positive = held.tile([rows, PIECE], F32, name=f"positive{start}")
+            gap = held.tile([rows, PIECE], F32, name=f"gap{start}")
+            hinge = held.tile([rows, PIECE], F32, name=f"hinge{start}")
+            nc.sync.dma_start(positive[:], pos[:, start:stop])
+            picked = table[:].indirect(offsets[:, start // PER_COLUMN : stop // PER_COLUMN])
+            nc.vector.tensor_tensor(gap[:], picked, positive[:], mybir.AluOpType.subtract)
+            nc.scalar.activation(hinge[:], gap[:], mybir.ActivationFunctionType.Relu, bias=margin[:])
+            nc.sync.dma_start(out[:, start:stop], hinge[:])

@@ -2,27 +2,42 @@ import concourse.mybir as mybir
 
 F32, U16 = mybir.dt.float32, mybir.dt.uint16
 MARGIN = 0.5
-PIECE = 512
 PER_COLUMN = 16
+STEP = 128
+
+
+def piece_widths(count):
+    rising = []
+    while 2 * sum(rising) < count:
+        rising.append(STEP * (len(rising) + 1))
+    assert 2 * sum(rising) == count
+    return rising + rising[::-1]
 
 
 def tile_lookup_hinge_sub_out_kernel(tc, tab, pos, offs, out):
     nc = tc.nc
-    rows, width = tab.shape
+    rows, columns = tab.shape
     count = pos.shape[1]
     with tc.tile_pool(name="held", bufs=1) as held:
+        table = held.tile([rows, columns], F32, name="table")
         offsets = held.tile([rows, count // PER_COLUMN], U16, name="offsets")
-        table = held.tile([rows, width], F32, name="table")
         margin = held.tile([rows, 1], F32, name="margin")
-        nc.sync.dma_start(offsets[:], offs)
         nc.sync.dma_start(table[:], tab)
+        nc.sync.dma_start(offsets[:], offs)
         nc.vector.memset(margin[:], MARGIN)
-        for start in range(0, count, PIECE):
-            stop = start + PIECE
-            positive = held.tile([rows, PIECE], F32, name=f"positive{start}")
-            gap = held.tile([rows, PIECE], F32, name=f"gap{start}")
-            hinge = held.tile([rows, PIECE], F32, name=f"hinge{start}")
-            nc.sync.dma_start(positive[:], pos[:, start:stop])
+
+        pieces = []
+        start = 0
+        for width in piece_widths(count):
+            positive = held.tile([rows, width], F32, name=f"positive{start}")
+            nc.sync.dma_start(positive[:], pos[:, start : start + width])
+            pieces.append((start, width, positive))
+            start += width
+
+        for start, width, positive in pieces:
+            stop = start + width
+            gap = held.tile([rows, width], F32, name=f"gap{start}")
+            hinge = held.tile([rows, width], F32, name=f"hinge{start}")
             picked = table[:].indirect(offsets[:, start // PER_COLUMN : stop // PER_COLUMN])
             nc.vector.tensor_tensor(gap[:], picked, positive[:], mybir.AluOpType.subtract)
             nc.scalar.activation(hinge[:], gap[:], mybir.ActivationFunctionType.Relu, bias=margin[:])

@@ -3,15 +3,16 @@ import concourse.mybir as mybir
 F32, U16 = mybir.dt.float32, mybir.dt.uint16
 MARGIN = 0.5
 PER_COLUMN = 16
-STEP = 128
+UNIT = 64
 
 
 def piece_widths(count):
-    rising = []
-    while 2 * sum(rising) < count:
-        rising.append(STEP * (len(rising) + 1))
-    assert 2 * sum(rising) == count
-    return rising + rising[::-1]
+    opening = [2 * UNIT, 4 * UNIT]
+    closing = [3 * UNIT, 2 * UNIT]
+    while sum(opening) + sum(closing) < count:
+        closing = [closing[0] + closing[1]] + closing
+    assert sum(opening) + sum(closing) == count
+    return opening + closing
 
 
 def tile_lookup_hinge_sub_out_kernel(tc, tab, pos, offs, out):
@@ -40,5 +41,8 @@ def tile_lookup_hinge_sub_out_kernel(tc, tab, pos, offs, out):
             hinge = held.tile([rows, width], F32, name=f"hinge{start}")
             picked = table[:].indirect(offsets[:, start // PER_COLUMN : stop // PER_COLUMN])
             nc.vector.tensor_tensor(gap[:], picked, positive[:], mybir.AluOpType.subtract)
-            nc.scalar.activation(hinge[:], gap[:], mybir.ActivationFunctionType.Relu, bias=margin[:])
+            if stop < count:
+                nc.scalar.activation(hinge[:], gap[:], mybir.ActivationFunctionType.Relu, bias=margin[:])
+            else:
+                nc.vector.tensor_scalar(hinge[:], gap[:], MARGIN, 0.0, mybir.AluOpType.add, mybir.AluOpType.max)
             nc.sync.dma_start(out[:, start:stop], hinge[:])

import concourse.mybir as mybir

F32, U16 = mybir.dt.float32, mybir.dt.uint16
MARGIN = 0.5
PER_COLUMN = 16
UNIT = 64


def piece_widths(count):
    opening = [2 * UNIT, 4 * UNIT]
    closing = [3 * UNIT, 2 * UNIT]
    while sum(opening) + sum(closing) < count:
        closing = [closing[0] + closing[1]] + closing
    assert sum(opening) + sum(closing) == count
    return opening + closing


def tile_lookup_hinge_sub_out_kernel(tc, tab, pos, offs, out):
    nc = tc.nc
    rows, columns = tab.shape
    count = pos.shape[1]
    with tc.tile_pool(name="held", bufs=1) as held:
        table = held.tile([rows, columns], F32, name="table")
        offsets = held.tile([rows, count // PER_COLUMN], U16, name="offsets")
        margin = held.tile([rows, 1], F32, name="margin")
        nc.sync.dma_start(table[:], tab)
        nc.sync.dma_start(offsets[:], offs)
        nc.vector.memset(margin[:], MARGIN)

        pieces = []
        start = 0
        for width in piece_widths(count):
            positive = held.tile([rows, width], F32, name=f"positive{start}")
            nc.sync.dma_start(positive[:], pos[:, start : start + width])
            pieces.append((start, width, positive))
            start += width

        for start, width, positive in pieces:
            stop = start + width
            gap = held.tile([rows, width], F32, name=f"gap{start}")
            hinge = held.tile([rows, width], F32, name=f"hinge{start}")
            picked = table[:].indirect(offsets[:, start // PER_COLUMN : stop // PER_COLUMN])
            nc.vector.tensor_tensor(gap[:], picked, positive[:], mybir.AluOpType.subtract)
            if stop < count:
                nc.scalar.activation(hinge[:], gap[:], mybir.ActivationFunctionType.Relu, bias=margin[:])
            else:
                nc.vector.tensor_scalar(hinge[:], gap[:], MARGIN, 0.0, mybir.AluOpType.add, mybir.AluOpType.max)
            nc.sync.dma_start(out[:, start:stop], hinge[:])
